import numpy as np
import ml_dtypes


def mxq(x, axis, fmt="e4m3"):
    dtype, down = {"e4m3": (ml_dtypes.float8_e4m3fn, 7), "e5m2": (ml_dtypes.float8_e5m2, 14)}[fmt]
    v = np.moveaxis(np.asarray(x, np.float32).astype(ml_dtypes.bfloat16).astype(np.float64), axis, -1)
    blocks = v.reshape(v.shape[:-1] + (-1, 32))
    amax = np.abs(blocks).max(-1, keepdims=True)
    byte = np.maximum(np.where(amax > 0, np.frexp(amax)[1] - 1 + 127, 0) - down, 1)
    scale = np.exp2(byte - 127.0)
    codes = (blocks / scale).astype(np.float32).astype(dtype).astype(np.float64)
    return np.moveaxis((codes * scale).reshape(v.shape), -1, axis)


WIDE = False


def mx_kscale(k):
    if not WIDE:
        return np.ones(k)
    levels = np.array([10, -10, 5, -5, 0])
    if k % 512:
        return np.exp2(np.random.permutation(np.resize(levels, k // 32))).repeat(32)
    a = np.empty((k // 512, 16))
    for p in range(k // 512):
        a[p, :8] = np.random.permutation(np.resize(levels, 8))
        for g in range(8):
            far = levels[np.abs(levels - a[p, g]) >= 10]
            a[p, g + 8] = far[np.random.randint(len(far))]
    return np.exp2(a.ravel()).repeat(32)


def f64(x):
    return np.asarray(x).astype(np.float64)


def striped(idx):
    return np.tile(np.asarray(idx).reshape(-1, 16).T, (8, 1)).astype(np.uint16)


def unstriped(offs):
    return offs[:16].T.reshape(-1).astype(np.int64)


E2M1 = np.array([0.0, 0.5, 1.0, 1.5, 2.0, 3.0, 4.0, 6.0, -0.0, -0.5, -1.0, -1.5, -2.0, -3.0, -4.0, -6.0])


def pack_weight(w, fmt):
    k, n = w.shape
    w = f64(np.asarray(w, np.float32).astype(ml_dtypes.bfloat16)).reshape(k // 32, 32, n)
    amax = np.abs(w).max(1)
    if fmt == "e4m3":
        byte = np.frexp(amax)[1] - 1 + 127 - 7
    else:
        mant, ex = np.frexp(amax / 6.0)
        byte = np.where(mant > 0.5, ex, ex - 1) + 127
    byte = np.clip(np.where(amax > 0, byte, 1), 1, 254)
    scaled = (w * np.exp2(127.0 - byte)[:, None, :]).reshape(k, n).astype(np.float32)
    by_word = np.ascontiguousarray(scaled.reshape(k // 512, 128, 4, n).transpose(0, 1, 3, 2))
    if fmt == "e4m3":
        words = by_word.astype(ml_dtypes.float8_e4m3fn).view(np.uint8)
    else:
        c = by_word.astype(ml_dtypes.float4_e2m1fn).view(np.uint8) & 0xF
        words = (c[..., 0::2] | (c[..., 1::2] << 4)).reshape(k // 512, 128, 2 * n)
    return np.ascontiguousarray(words), np.ascontiguousarray(byte.astype(np.uint8).reshape(k // 512, 16, n))


def unpack_weight(words, scales, fmt):
    g, _, n = scales.shape
    words = np.ascontiguousarray(words).reshape(g, 128, n, -1)
    if fmt == "e4m3":
        vals = words.view(ml_dtypes.float8_e4m3fn).astype(np.float64)
    else:
        nib = np.empty((g, 128, n, 4), np.uint8)
        nib[..., 0::2] = words & 0xF
        nib[..., 1::2] = words >> 4
        vals = E2M1[nib]
    vals = vals * np.repeat(np.exp2(scales.astype(np.float64) - 127.0), 8, axis=1)[..., None]
    return vals.transpose(0, 1, 3, 2).reshape(g * 512, n)


D, K, T, U, I, Q = 1024, 512, 2048, 2048, 512, 128


def setup_inputs():
    n = np.random.standard_normal
    idx = np.random.permutation(T)[:I]
    idx2 = np.random.permutation(U)[:I]
    fd = mx_kscale(D)
    fk = mx_kscale(K)
    vfp = pack_weight(n((D, T)) / fd[:, None], "e2m1")
    vcp = pack_weight(n((K, U)) / fk[:, None], "e4m3")
    return {
        "hf": (n((D, Q)) * 1.0 / np.sqrt(D) * fd[:, None]).astype(np.float32),
        "hc": (n((K, Q)) * 1.0 / np.sqrt(K) * fk[:, None]).astype(np.float32),
        "vf_words": vfp[0],
        "vf_scales": vfp[1],
        "vc_words": vcp[0],
        "vc_scales": vcp[1],
        "la": (np.random.uniform(0.5, 1.5, (Q, 1))).astype(np.float32),
        "lb": (np.random.uniform(0.5, 1.5, (Q, 1))).astype(np.float32),
        "wa": (np.random.uniform(0.5, 1.0, (Q, 1))).astype(np.float32),
        "wb": (np.random.uniform(0.2, 0.8, (Q, 1))).astype(np.float32),
        "offs": striped(idx),
        "offs2": striped(idx2),
    }


def reference(hf, hc, vf_words, vf_scales, vc_words, vc_scales, la, lb, wa, wb, offs, offs2):
    idx = unstriped(offs)
    idx2 = unstriped(offs2)
    vfu = unpack_weight(vf_words, vf_scales, "e2m1")
    vcu = unpack_weight(vc_words, vc_scales, "e4m3")
    hfq = mxq(f64(hf), 0, "e4m3")
    vfidxg = vfu[:, idx]
    a = hfq.T @ vfidxg
    hcq = mxq(f64(hc), 0, "e4m3")
    vcidx2g = vcu[:, idx2]
    b = hcq.T @ vcidx2g
    y = f64(wa) * (a - f64(la)) + f64(wb) * (b - f64(lb))
    return y

@@ -1,0 +1,140 @@
+from contextlib import ExitStack
+
+import concourse.mybir as mybir
+
+D, K, T, I, Q = 1024, 512, 2048, 512, 128
+FLOPS = 2 * Q * I * (D + K)
+
+F32 = mybir.dt.float32
+BF16 = mybir.dt.bfloat16
+I32 = mybir.dt.int32
+U32 = mybir.dt.uint32
+U16 = mybir.dt.uint16
+U8 = mybir.dt.uint8
+FP8X4 = mybir.dt.float8_e4m3fn_x4
+FP4X4 = mybir.dt.float4_e2m1fn_x4
+MULT = mybir.AluOpType.mult
+ADD = mybir.AluOpType.add
+SUBTRACT = mybir.AluOpType.subtract
+IDENTITY = mybir.ActivationFunctionType.Identity
+
+P = 128
+PACK = 4
+F_PASSES = D // (P * PACK)
+HALF = I // 2
+
+
+def cast_and_interleave(nc, grouped, raw):
+    nc.scalar.copy(
+        out=grouped.rearrange("p (c i) t -> p c t i", i=4),
+        in_=raw.rearrange("p t (c i) -> p c t i", i=4),
+    )
+
+
+def tile_attend_noisychannel_kernel(tc, hf, hc, vf_words, vf_scales, vc_words, vc_scales, la, lb, wa, wb, offs, offs2, out):
+    nc = tc.nc
+    with ExitStack() as ctx:
+        sb = ctx.enter_context(tc.tile_pool(name="sb", bufs=1))
+        psum = ctx.enter_context(tc.psum_pool(name="psum", bufs=1))
+
+        f_list = sb.tile([P, I // 16], U16, name="f_list")
+        c_list = sb.tile([P, I // 16], U16, name="c_list")
+        f_scale_table = sb.tile([P, T], U8, name="f_scale_table", tag="shared", align_bytes=64)
+        c_scale_table = sb.tile([P, T], U8, name="c_scale_table", align_bytes=64)
+        f_tables = [sb.tile([P, T], U16, name="f_table%d" % z, align_bytes=64) for z in range(F_PASSES)]
+        hf_raw = sb.tile([P, F_PASSES, PACK, Q], F32, name="hf_raw", align_bytes=64)
+        hc_raw = sb.tile([P, PACK, Q], F32, name="hc_raw", align_bytes=64)
+        f_planes = sb.tile([P, F_PASSES * I], U8, name="f_planes", align_bytes=64)
+
+        nc.vector.memset(c_scale_table[:].bitcast(I32), 0)
+        nc.vector.memset(f_scale_table[32:64, :].bitcast(I32), 0)
+        nc.vector.memset(f_scale_table[64:128, :].bitcast(I32), 0)
+        nc.vector.memset(f_planes[:].bitcast(I32), 0)
+        warm_in = sb.tile([P, 1], F32, name="warm_in")
+        warm_out = sb.tile([P, 1], F32, name="warm_out")
+        nc.vector.memset(warm_in[:], 0.0)
+
+        nc.sync.dma_start(f_list[:], offs)
+        nc.sync.dma_start(f_scale_table[0:32, :].bitcast(I32), vf_scales.rearrange("z f c -> f z c").bitcast(I32))
+        nc.sync.dma_start(c_list[:], offs2)
+        nc.sync.dma_start(f_tables[0][:].bitcast(I32), vf_words[0].bitcast(I32))
+        nc.sync.dma_start(hf_raw[:], hf.rearrange("(z p t) q -> p z t q", z=F_PASSES, t=PACK))
+        nc.sync.dma_start(f_tables[1][:].bitcast(I32), vf_words[1].bitcast(I32))
+        nc.sync.dma_start(hc_raw[:], hc.rearrange("(p t) q -> p t q", t=PACK))
+        for g in range(4):
+            nc.scalar.dma_start(
+                c_scale_table[32 * g : 32 * g + 4, :].bitcast(I32), vc_scales[0, 4 * g : 4 * g + 4, :].bitcast(I32)
+            )
+        nc.scalar.copy(warm_out[:], warm_in[:])
+        la_col = sb.tile([P, 1], F32, name="la_col")
+        lb_col = sb.tile([P, 1], F32, name="lb_col")
+        wa_col = sb.tile([P, 1], F32, name="wa_col")
+        wb_col = sb.tile([P, 1], F32, name="wb_col")
+        for col, src in ((wa_col, wa), (la_col, la), (wb_col, wb), (lb_col, lb)):
+            nc.gpsimd.dma_start(col[:], src)
+
+        f_scale_rows = sb.tile([P, I], U8, name="f_scale_rows", align_bytes=64)
+        nc.vector.tensor_copy(f_scale_rows[:], f_scale_table[:].indirect(f_list[:]))
+        c_table = sb.tile([P, T], U32, name="c_table", tag="shared", align_bytes=64)
+        nc.sync.dma_start(c_table[:].bitcast(I32), vc_words[0].rearrange("p c t -> p (c t)").bitcast(I32))
+        for g in range(4):
+            nc.scalar.dma_start(
+                f_planes[32 * g : 32 * g + 4, :].bitcast(I32), f_scale_rows[8 * g : 8 * g + 8, :].bitcast(I32)
+            )
+
+        f_words = [sb.tile([P, I], U16, name="f_words%d" % z, align_bytes=64) for z in range(F_PASSES)]
+        c_plane = sb.tile([P, I], U8, name="c_plane", align_bytes=64)
+        nc.vector.tensor_copy(f_words[0][:], f_tables[0][:].indirect(f_list[:]))
+        nc.vector.tensor_copy(c_plane[:], c_scale_table[:].indirect(c_list[:]))
+        nc.vector.tensor_copy(f_words[1][:], f_tables[1][:].indirect(f_list[:]))
+
+        hf_grouped = sb.tile([P, F_PASSES, Q, PACK], BF16, name="hf_grouped", align_bytes=64)
+        hc_grouped = sb.tile([P, Q, PACK], BF16, name="hc_grouped", align_bytes=64)
+        for z in range(F_PASSES):
+            cast_and_interleave(nc, hf_grouped[:, z], hf_raw[:, z])
+        cast_and_interleave(nc, hc_grouped[:], hc_raw[:])
+        hf_codes = sb.tile([P, F_PASSES * Q], U32, name="hf_codes", align_bytes=64)
+        hf_plane = sb.tile([P, F_PASSES * Q], U8, name="hf_plane", align_bytes=64)
+        hc_codes = sb.tile([P, Q], U32, name="hc_codes", align_bytes=64)
+        hc_plane = sb.tile([P, Q], U8, name="hc_plane", align_bytes=64)
+        nc.vector.quantize_mx(hf_codes[:].bitcast(FP8X4), hf_plane[:], hf_grouped[:].rearrange("p z q t -> p (z q t)"))
+        nc.vector.quantize_mx(hc_codes[:].bitcast(FP8X4), hc_plane[:], hc_grouped[:].rearrange("p q t -> p (q t)"))
+
+        a_acc = psum.tile([P, I], F32, name="a_acc")
+        for z in range(F_PASSES):
+            nc.tensor.matmul_mx(
+                out=a_acc[:],
+                lhsT=hf_codes[:, z * Q : (z + 1) * Q].bitcast(FP8X4),
+                lhsT_scale=hf_plane[:, z * Q : (z + 1) * Q],
+                rhs=f_words[z][:].bitcast(FP4X4),
+                rhs_scale=f_planes[:, z * I : (z + 1) * I],
+                start=(z == 0),
+                stop=(z == F_PASSES - 1),
+            )
+
+        neg_wa_la = sb.tile([P, 1], F32, name="neg_wa_la")
+        wb_lb = sb.tile([P, 1], F32, name="wb_lb")
+        offset = sb.tile([P, 1], F32, name="offset")
+        nc.gpsimd.tensor_scalar(neg_wa_la[:], la_col[:], wa_col[:], -1.0, MULT, MULT)
+        nc.gpsimd.tensor_tensor(wb_lb[:], lb_col[:], wb_col[:], MULT)
+        nc.gpsimd.tensor_tensor(offset[:], neg_wa_la[:], wb_lb[:], SUBTRACT)
+        a_term = sb.tile([P, I], F32, name="a_term")
+        nc.scalar.activation(a_term[:], a_acc[:], IDENTITY, bias=offset[:], scale=wa_col[:])
+
+        for h in range(2):
+            cols = slice(h * HALF, (h + 1) * HALF)
+            c_words = sb.tile([P, HALF], U32, name="c_words%d" % h, align_bytes=64)
+            nc.vector.tensor_copy(c_words[:], c_table[:].indirect(c_list[:, h * HALF // 16 : (h + 1) * HALF // 16]))
+            b_acc = psum.tile([P, HALF], F32, name="b_acc%d" % h)
+            nc.tensor.matmul_mx(
+                out=b_acc[:],
+                lhsT=hc_codes[:].bitcast(FP8X4),
+                lhsT_scale=hc_plane[:],
+                rhs=c_words[:].bitcast(FP8X4),
+                rhs_scale=c_plane[:, cols],
+                start=True,
+                stop=True,
+            )
+            y = sb.tile([P, HALF], F32, name="y%d" % h)
+            nc.vector.scalar_tensor_tensor(y[:], b_acc[:], wb_col[:], a_term[:, cols], MULT, ADD)
+            (nc.sync if h == 0 else nc.scalar).dma_start(out[:, cols], y[:])

@@ -15,7 +15,6 @@ FP8X4 = mybir.dt.float8_e4m3fn_x4
 FP4X4 = mybir.dt.float4_e2m1fn_x4
 MULT = mybir.AluOpType.mult
 ADD = mybir.AluOpType.add
-SUBTRACT = mybir.AluOpType.subtract
 IDENTITY = mybir.ActivationFunctionType.Identity
 
 P = 128
@@ -41,31 +40,22 @@ def tile_attend_noisychannel_kernel(tc, hf, hc, vf_words, vf_scales, vc_words, v
         c_list = sb.tile([P, I // 16], U16, name="c_list")
         f_scale_table = sb.tile([P, T], U8, name="f_scale_table", tag="shared", align_bytes=64)
         c_scale_table = sb.tile([P, T], U8, name="c_scale_table", align_bytes=64)
-        f_tables = [sb.tile([P, T], U16, name="f_table%d" % z, align_bytes=64) for z in range(F_PASSES)]
+        f_tables = [sb.tile([P, T], U16, name="f_table%d" % z, tag="f_table%d" % z, align_bytes=64) for z in range(F_PASSES)]
         hf_raw = sb.tile([P, F_PASSES, PACK, Q], F32, name="hf_raw", align_bytes=64)
-        hc_raw = sb.tile([P, PACK, Q], F32, name="hc_raw", align_bytes=64)
+        hc_raw = sb.tile([P, PACK, Q], F32, name="hc_raw", tag="late2", align_bytes=64)
         f_planes = sb.tile([P, F_PASSES * I], U8, name="f_planes", align_bytes=64)
 
         nc.vector.memset(c_scale_table[:].bitcast(I32), 0)
-        nc.vector.memset(f_scale_table[32:64, :].bitcast(I32), 0)
-        nc.vector.memset(f_scale_table[64:128, :].bitcast(I32), 0)
-        nc.vector.memset(f_planes[:].bitcast(I32), 0)
-        warm_in = sb.tile([P, 1], F32, name="warm_in")
-        warm_out = sb.tile([P, 1], F32, name="warm_out")
-        nc.vector.memset(warm_in[:], 0.0)
+        nc.vector.memset(f_scale_table[0:96, :].bitcast(I32), 0)
 
         nc.sync.dma_start(f_list[:], offs)
-        nc.sync.dma_start(f_scale_table[0:32, :].bitcast(I32), vf_scales.rearrange("z f c -> f z c").bitcast(I32))
+        nc.sync.dma_start(f_scale_table[96:128, :].bitcast(I32), vf_scales.rearrange("z f c -> f z c").bitcast(I32))
         nc.sync.dma_start(c_list[:], offs2)
         nc.sync.dma_start(f_tables[0][:].bitcast(I32), vf_words[0].bitcast(I32))
-        nc.sync.dma_start(hf_raw[:], hf.rearrange("(z p t) q -> p z t q", z=F_PASSES, t=PACK))
         nc.sync.dma_start(f_tables[1][:].bitcast(I32), vf_words[1].bitcast(I32))
+        nc.sync.dma_start(hf_raw[:], hf.rearrange("(z p t) q -> p z t q", z=F_PASSES, t=PACK))
         nc.sync.dma_start(hc_raw[:], hc.rearrange("(p t) q -> p t q", t=PACK))
-        for g in range(4):
-            nc.scalar.dma_start(
-                c_scale_table[32 * g : 32 * g + 4, :].bitcast(I32), vc_scales[0, 4 * g : 4 * g + 4, :].bitcast(I32)
-            )
-        nc.scalar.copy(warm_out[:], warm_in[:])
+        nc.scalar.dma_start(c_scale_table[0:128:8, :].bitcast(I32), vc_scales[0].bitcast(I32))
         la_col = sb.tile([P, 1], F32, name="la_col")
         lb_col = sb.tile([P, 1], F32, name="lb_col")
         wa_col = sb.tile([P, 1], F32, name="wa_col")
@@ -75,18 +65,21 @@ def tile_attend_noisychannel_kernel(tc, hf, hc, vf_words, vf_scales, vc_words, v
 
         f_scale_rows = sb.tile([P, I], U8, name="f_scale_rows", align_bytes=64)
         nc.vector.tensor_copy(f_scale_rows[:], f_scale_table[:].indirect(f_list[:]))
+        for g in (0, 2, 1, 3):
+            nc.sync.dma_start(
+                f_planes[32 * g : 32 * g + 4, :].bitcast(I32), f_scale_rows[96 + 8 * g : 96 + 8 * g + 8, :].bitcast(I32)
+            )
         c_table = sb.tile([P, T], U32, name="c_table", tag="shared", align_bytes=64)
         nc.sync.dma_start(c_table[:].bitcast(I32), vc_words[0].rearrange("p c t -> p (c t)").bitcast(I32))
-        for g in range(4):
-            nc.scalar.dma_start(
-                f_planes[32 * g : 32 * g + 4, :].bitcast(I32), f_scale_rows[8 * g : 8 * g + 8, :].bitcast(I32)
-            )
 
         f_words = [sb.tile([P, I], U16, name="f_words%d" % z, align_bytes=64) for z in range(F_PASSES)]
         c_plane = sb.tile([P, I], U8, name="c_plane", align_bytes=64)
         nc.vector.tensor_copy(f_words[0][:], f_tables[0][:].indirect(f_list[:]))
-        nc.vector.tensor_copy(c_plane[:], c_scale_table[:].indirect(c_list[:]))
         nc.vector.tensor_copy(f_words[1][:], f_tables[1][:].indirect(f_list[:]))
+        c_scale_rows = sb.tile([P, I], U8, name="c_scale_rows", tag="f_table1", align_bytes=64)
+        nc.vector.tensor_copy(c_scale_rows[:], c_scale_table[:].indirect(c_list[:]))
+        for r in range(4):
+            nc.sync.dma_start(c_plane[r:128:32, :].bitcast(I32), c_scale_rows[8 * r : 128 : 32, :].bitcast(I32))
 
         hf_grouped = sb.tile([P, F_PASSES, Q, PACK], BF16, name="hf_grouped", align_bytes=64)
         hc_grouped = sb.tile([P, Q, PACK], BF16, name="hc_grouped", align_bytes=64)
@@ -112,12 +105,12 @@ def tile_attend_noisychannel_kernel(tc, hf, hc, vf_words, vf_scales, vc_words, v
                 stop=(z == F_PASSES - 1),
             )
 
-        neg_wa_la = sb.tile([P, 1], F32, name="neg_wa_la")
-        wb_lb = sb.tile([P, 1], F32, name="wb_lb")
+        wb_lb = sb.tile([P, 1], F32, name="wb_lb", tag="late2", align_bytes=64)
+        both = sb.tile([P, 1], F32, name="both")
         offset = sb.tile([P, 1], F32, name="offset")
-        nc.gpsimd.tensor_scalar(neg_wa_la[:], la_col[:], wa_col[:], -1.0, MULT, MULT)
-        nc.gpsimd.tensor_tensor(wb_lb[:], lb_col[:], wb_col[:], MULT)
-        nc.gpsimd.tensor_tensor(offset[:], neg_wa_la[:], wb_lb[:], SUBTRACT)
+        nc.scalar.activation(wb_lb[:], lb_col[:], IDENTITY, scale=wb_col[:])
+        nc.scalar.activation(both[:], la_col[:], IDENTITY, bias=wb_lb[:], scale=wa_col[:])
+        nc.scalar.activation(offset[:], both[:], IDENTITY, scale=-1.0)
         a_term = sb.tile([P, I], F32, name="a_term")
         nc.scalar.activation(a_term[:], a_acc[:], IDENTITY, bias=offset[:], scale=wa_col[:])
 

@@ -41,7 +41,7 @@ def tile_attend_noisychannel_kernel(tc, hf, hc, vf_words, vf_scales, vc_words, v
         f_scale_table = sb.tile([P, T], U8, name="f_scale_table", tag="shared", align_bytes=64)
         c_scale_table = sb.tile([P, T], U8, name="c_scale_table", align_bytes=64)
         f_tables = [sb.tile([P, T], U16, name="f_table%d" % z, tag="f_table%d" % z, align_bytes=64) for z in range(F_PASSES)]
-        hf_raw = sb.tile([P, F_PASSES, PACK, Q], F32, name="hf_raw", align_bytes=64)
+        hf_raw = sb.tile([P, F_PASSES, PACK, Q], F32, name="hf_raw", tag="hf_raw", align_bytes=64)
         hc_raw = sb.tile([P, PACK, Q], F32, name="hc_raw", tag="late2", align_bytes=64)
         f_planes = sb.tile([P, F_PASSES * I], U8, name="f_planes", align_bytes=64)
 
@@ -49,9 +49,9 @@ def tile_attend_noisychannel_kernel(tc, hf, hc, vf_words, vf_scales, vc_words, v
         nc.vector.memset(f_scale_table[0:96, :].bitcast(I32), 0)
 
         nc.sync.dma_start(f_list[:], offs)
-        nc.sync.dma_start(f_scale_table[96:128, :].bitcast(I32), vf_scales.rearrange("z f c -> f z c").bitcast(I32))
-        nc.sync.dma_start(c_list[:], offs2)
+        nc.scalar.dma_start(f_scale_table[96:128, :].bitcast(I32), vf_scales.rearrange("z f c -> f z c").bitcast(I32))
         nc.sync.dma_start(f_tables[0][:].bitcast(I32), vf_words[0].bitcast(I32))
+        nc.sync.dma_start(c_list[:], offs2)
         nc.sync.dma_start(f_tables[1][:].bitcast(I32), vf_words[1].bitcast(I32))
         nc.sync.dma_start(hf_raw[:], hf.rearrange("(z p t) q -> p z t q", z=F_PASSES, t=PACK))
         nc.sync.dma_start(hc_raw[:], hc.rearrange("(p t) q -> p t q", t=PACK))
@@ -73,18 +73,18 @@ def tile_attend_noisychannel_kernel(tc, hf, hc, vf_words, vf_scales, vc_words, v
         nc.sync.dma_start(c_table[:].bitcast(I32), vc_words[0].rearrange("p c t -> p (c t)").bitcast(I32))
 
         f_words = [sb.tile([P, I], U16, name="f_words%d" % z, align_bytes=64) for z in range(F_PASSES)]
-        c_plane = sb.tile([P, I], U8, name="c_plane", align_bytes=64)
         nc.vector.tensor_copy(f_words[0][:], f_tables[0][:].indirect(f_list[:]))
-        nc.vector.tensor_copy(f_words[1][:], f_tables[1][:].indirect(f_list[:]))
-        c_scale_rows = sb.tile([P, I], U8, name="c_scale_rows", tag="f_table1", align_bytes=64)
+        c_scale_rows = sb.tile([P, I], U8, name="c_scale_rows", tag="f_table0", align_bytes=64)
         nc.vector.tensor_copy(c_scale_rows[:], c_scale_table[:].indirect(c_list[:]))
-        for r in range(4):
-            nc.sync.dma_start(c_plane[r:128:32, :].bitcast(I32), c_scale_rows[8 * r : 128 : 32, :].bitcast(I32))
+        nc.vector.tensor_copy(f_words[1][:], f_tables[1][:].indirect(f_list[:]))
 
         hf_grouped = sb.tile([P, F_PASSES, Q, PACK], BF16, name="hf_grouped", align_bytes=64)
         hc_grouped = sb.tile([P, Q, PACK], BF16, name="hc_grouped", align_bytes=64)
         for z in range(F_PASSES):
             cast_and_interleave(nc, hf_grouped[:, z], hf_raw[:, z])
+        c_plane = sb.tile([P, I], U8, name="c_plane", tag="hf_raw", align_bytes=64)
+        for r in range(4):
+            nc.scalar.dma_start(c_plane[r:128:32, :].bitcast(I32), c_scale_rows[8 * r : 128 : 32, :].bitcast(I32))
         cast_and_interleave(nc, hc_grouped[:], hc_raw[:])
         hf_codes = sb.tile([P, F_PASSES * Q], U32, name="hf_codes", align_bytes=64)
         hf_plane = sb.tile([P, F_PASSES * Q], U8, name="hf_plane", align_bytes=64)

@@ -52,8 +52,8 @@ def tile_attend_noisychannel_kernel(tc, hf, hc, vf_words, vf_scales, vc_words, v
         nc.scalar.dma_start(f_scale_table[96:128, :].bitcast(I32), vf_scales.rearrange("z f c -> f z c").bitcast(I32))
         nc.sync.dma_start(f_tables[0][:].bitcast(I32), vf_words[0].bitcast(I32))
         nc.sync.dma_start(c_list[:], offs2)
-        nc.sync.dma_start(f_tables[1][:].bitcast(I32), vf_words[1].bitcast(I32))
         nc.sync.dma_start(hf_raw[:], hf.rearrange("(z p t) q -> p z t q", z=F_PASSES, t=PACK))
+        nc.sync.dma_start(f_tables[1][:].bitcast(I32), vf_words[1].bitcast(I32))
         nc.sync.dma_start(hc_raw[:], hc.rearrange("(p t) q -> p t q", t=PACK))
         nc.scalar.dma_start(c_scale_table[0:128:8, :].bitcast(I32), vc_scales[0].bitcast(I32))
         la_col = sb.tile([P, 1], F32, name="la_col")
@@ -114,20 +114,21 @@ def tile_attend_noisychannel_kernel(tc, hf, hc, vf_words, vf_scales, vc_words, v
         a_term = sb.tile([P, I], F32, name="a_term")
         nc.scalar.activation(a_term[:], a_acc[:], IDENTITY, bias=offset[:], scale=wa_col[:])
 
+        c_words = [sb.tile([P, HALF], U32, name="c_words%d" % h, align_bytes=64) for h in range(2)]
         for h in range(2):
-            cols = slice(h * HALF, (h + 1) * HALF)
-            c_words = sb.tile([P, HALF], U32, name="c_words%d" % h, align_bytes=64)
-            nc.vector.tensor_copy(c_words[:], c_table[:].indirect(c_list[:, h * HALF // 16 : (h + 1) * HALF // 16]))
-            b_acc = psum.tile([P, HALF], F32, name="b_acc%d" % h)
+            nc.vector.tensor_copy(c_words[h][:], c_table[:].indirect(c_list[:, h * HALF // 16 : (h + 1) * HALF // 16]))
+        for j, (start, width) in enumerate(((0, HALF), (HALF, HALF // 2), (HALF + HALF // 2, HALF // 2))):
+            cols = slice(start, start + width)
+            b_acc = psum.tile([P, width], F32, name="b_acc%d" % j)
             nc.tensor.matmul_mx(
                 out=b_acc[:],
                 lhsT=hc_codes[:].bitcast(FP8X4),
                 lhsT_scale=hc_plane[:],
-                rhs=c_words[:].bitcast(FP8X4),
+                rhs=c_words[start // HALF][:, start % HALF : start % HALF + width].bitcast(FP8X4),
                 rhs_scale=c_plane[:, cols],
                 start=True,
                 stop=True,
             )
-            y = sb.tile([P, HALF], F32, name="y%d" % h)
+            y = sb.tile([P, width], F32, name="y%d" % j)
             nc.vector.scalar_tensor_tensor(y[:], b_acc[:], wb_col[:], a_term[:, cols], MULT, ADD)
-            (nc.sync if h == 0 else nc.scalar).dma_start(out[:, cols], y[:])
+            (nc.scalar if j == 1 else nc.sync).dma_start(out[:, cols], y[:])

@@ -19,8 +19,13 @@ IDENTITY = mybir.ActivationFunctionType.Identity
 
 P = 128
 PACK = 4
+QUADRANT = 32
 F_PASSES = D // (P * PACK)
+LIST_ROWS = 16
 HALF = I // 2
+F_ROWS_FROM = P - QUADRANT
+C_ROWS_FROM, C_ROWS_STEP = 4, 8
+PIECES = ((0, HALF), (HALF, HALF // 2), (HALF + HALF // 2, HALF // 2))
 
 
 def cast_and_interleave(nc, grouped, raw):
@@ -36,40 +41,45 @@ def tile_attend_noisychannel_kernel(tc, hf, hc, vf_words, vf_scales, vc_words, v
         sb = ctx.enter_context(tc.tile_pool(name="sb", bufs=1))
         psum = ctx.enter_context(tc.psum_pool(name="psum", bufs=1))
 
-        f_list = sb.tile([P, I // 16], U16, name="f_list")
-        c_list = sb.tile([P, I // 16], U16, name="c_list")
-        f_scale_table = sb.tile([P, T], U8, name="f_scale_table", tag="shared", align_bytes=64)
+        f_list = sb.tile([P, I // LIST_ROWS], U16, name="f_list")
+        c_list = sb.tile([P, I // LIST_ROWS], U16, name="c_list")
+        f_scale_table = sb.tile([P, T], U8, name="f_scale_table", tag="f_scale_table", align_bytes=64)
         c_scale_table = sb.tile([P, T], U8, name="c_scale_table", align_bytes=64)
         f_tables = [sb.tile([P, T], U16, name="f_table%d" % z, tag="f_table%d" % z, align_bytes=64) for z in range(F_PASSES)]
         hf_raw = sb.tile([P, F_PASSES, PACK, Q], F32, name="hf_raw", tag="hf_raw", align_bytes=64)
-        hc_raw = sb.tile([P, PACK, Q], F32, name="hc_raw", tag="late2", align_bytes=64)
+        hc_raw = sb.tile([P, PACK, Q], F32, name="hc_raw", tag="hc_raw", align_bytes=64)
         f_planes = sb.tile([P, F_PASSES * I], U8, name="f_planes", align_bytes=64)
 
         nc.vector.memset(c_scale_table[:].bitcast(I32), 0)
-        nc.vector.memset(f_scale_table[0:96, :].bitcast(I32), 0)
+        nc.vector.memset(f_scale_table[0:F_ROWS_FROM, :].bitcast(I32), 0)
 
-        nc.sync.dma_start(f_list[:], offs)
-        nc.scalar.dma_start(f_scale_table[96:128, :].bitcast(I32), vf_scales.rearrange("z f c -> f z c").bitcast(I32))
-        nc.sync.dma_start(f_tables[0][:].bitcast(I32), vf_words[0].bitcast(I32))
-        nc.sync.dma_start(c_list[:], offs2)
-        nc.sync.dma_start(hf_raw[:], hf.rearrange("(z p t) q -> p z t q", z=F_PASSES, t=PACK))
-        nc.sync.dma_start(f_tables[1][:].bitcast(I32), vf_words[1].bitcast(I32))
-        nc.sync.dma_start(hc_raw[:], hc.rearrange("(p t) q -> p t q", t=PACK))
-        nc.scalar.dma_start(c_scale_table[0:128:8, :].bitcast(I32), vc_scales[0].bitcast(I32))
         la_col = sb.tile([P, 1], F32, name="la_col")
         lb_col = sb.tile([P, 1], F32, name="lb_col")
         wa_col = sb.tile([P, 1], F32, name="wa_col")
         wb_col = sb.tile([P, 1], F32, name="wb_col")
-        for col, src in ((wa_col, wa), (la_col, la), (wb_col, wb), (lb_col, lb)):
-            nc.gpsimd.dma_start(col[:], src)
+        nc.sync.dma_start(f_list[:], offs)
+        nc.scalar.dma_start(f_scale_table[F_ROWS_FROM:P, :].bitcast(I32), vf_scales.rearrange("z f c -> f z c").bitcast(I32))
+        nc.sync.dma_start(f_tables[0][:].bitcast(I32), vf_words[0].bitcast(I32))
+        nc.sync.dma_start(c_list[:], offs2)
+        nc.sync.dma_start(wa_col[:], wa)
+        nc.sync.dma_start(la_col[:], la)
+        nc.sync.dma_start(lb_col[:], lb)
+        nc.sync.dma_start(hf_raw[:], hf.rearrange("(z p t) q -> p z t q", z=F_PASSES, t=PACK))
+        nc.sync.dma_start(f_tables[1][:].bitcast(I32), vf_words[1].bitcast(I32))
+        nc.sync.dma_start(hc_raw[:], hc.rearrange("(p t) q -> p t q", t=PACK))
+        nc.scalar.dma_start(c_scale_table[C_ROWS_FROM:P:C_ROWS_STEP, :].bitcast(I32), vc_scales[0].bitcast(I32))
+        nc.gpsimd.dma_start(wb_col[:], wb)
 
         f_scale_rows = sb.tile([P, I], U8, name="f_scale_rows", align_bytes=64)
         nc.vector.tensor_copy(f_scale_rows[:], f_scale_table[:].indirect(f_list[:]))
+        rows_a_move = PACK * F_PASSES
         for g in (0, 2, 1, 3):
+            first = F_ROWS_FROM + rows_a_move * g
             nc.sync.dma_start(
-                f_planes[32 * g : 32 * g + 4, :].bitcast(I32), f_scale_rows[96 + 8 * g : 96 + 8 * g + 8, :].bitcast(I32)
+                f_planes[QUADRANT * g : QUADRANT * g + 4, :].bitcast(I32),
+                f_scale_rows[first : first + rows_a_move, :].bitcast(I32),
             )
-        c_table = sb.tile([P, T], U32, name="c_table", tag="shared", align_bytes=64)
+        c_table = sb.tile([P, T], U32, name="c_table", tag="f_scale_table", align_bytes=64)
         nc.sync.dma_start(c_table[:].bitcast(I32), vc_words[0].rearrange("p c t -> p (c t)").bitcast(I32))
 
         f_words = [sb.tile([P, I], U16, name="f_words%d" % z, align_bytes=64) for z in range(F_PASSES)]
@@ -84,7 +94,10 @@ def tile_attend_noisychannel_kernel(tc, hf, hc, vf_words, vf_scales, vc_words, v
             cast_and_interleave(nc, hf_grouped[:, z], hf_raw[:, z])
         c_plane = sb.tile([P, I], U8, name="c_plane", tag="hf_raw", align_bytes=64)
         for r in range(4):
-            nc.scalar.dma_start(c_plane[r:128:32, :].bitcast(I32), c_scale_rows[8 * r : 128 : 32, :].bitcast(I32))
+            nc.scalar.dma_start(
+                c_plane[r:P:QUADRANT, :].bitcast(I32),
+                c_scale_rows[C_ROWS_FROM + C_ROWS_STEP * r : P : QUADRANT, :].bitcast(I32),
+            )
         cast_and_interleave(nc, hc_grouped[:], hc_raw[:])
         hf_codes = sb.tile([P, F_PASSES * Q], U32, name="hf_codes", align_bytes=64)
         hf_plane = sb.tile([P, F_PASSES * Q], U8, name="hf_plane", align_bytes=64)
@@ -105,19 +118,20 @@ def tile_attend_noisychannel_kernel(tc, hf, hc, vf_words, vf_scales, vc_words, v
                 stop=(z == F_PASSES - 1),
             )
 
-        wb_lb = sb.tile([P, 1], F32, name="wb_lb", tag="late2", align_bytes=64)
-        both = sb.tile([P, 1], F32, name="both")
-        offset = sb.tile([P, 1], F32, name="offset")
+        wb_lb = sb.tile([P, 1], F32, name="wb_lb", tag="hc_raw", align_bytes=64)
+        weighted_sums = sb.tile([P, 1], F32, name="weighted_sums")
+        bias_col = sb.tile([P, 1], F32, name="bias_col")
         nc.scalar.activation(wb_lb[:], lb_col[:], IDENTITY, scale=wb_col[:])
-        nc.scalar.activation(both[:], la_col[:], IDENTITY, bias=wb_lb[:], scale=wa_col[:])
-        nc.scalar.activation(offset[:], both[:], IDENTITY, scale=-1.0)
+        nc.scalar.activation(weighted_sums[:], la_col[:], IDENTITY, bias=wb_lb[:], scale=wa_col[:])
+        nc.scalar.activation(bias_col[:], weighted_sums[:], IDENTITY, scale=-1.0)
         a_term = sb.tile([P, I], F32, name="a_term")
-        nc.scalar.activation(a_term[:], a_acc[:], IDENTITY, bias=offset[:], scale=wa_col[:])
+        nc.scalar.activation(a_term[:], a_acc[:], IDENTITY, bias=bias_col[:], scale=wa_col[:])
 
         c_words = [sb.tile([P, HALF], U32, name="c_words%d" % h, align_bytes=64) for h in range(2)]
         for h in range(2):
-            nc.vector.tensor_copy(c_words[h][:], c_table[:].indirect(c_list[:, h * HALF // 16 : (h + 1) * HALF // 16]))
-        for j, (start, width) in enumerate(((0, HALF), (HALF, HALF // 2), (HALF + HALF // 2, HALF // 2))):
+            entries = c_list[:, h * HALF // LIST_ROWS : (h + 1) * HALF // LIST_ROWS]
+            nc.vector.tensor_copy(c_words[h][:], c_table[:].indirect(entries))
+        for j, (start, width) in enumerate(PIECES):
             cols = slice(start, start + width)
             b_acc = psum.tile([P, width], F32, name="b_acc%d" % j)
             nc.tensor.matmul_mx(
@@ -131,4 +145,4 @@ def tile_attend_noisychannel_kernel(tc, hf, hc, vf_words, vf_scales, vc_words, v
             )
             y = sb.tile([P, width], F32, name="y%d" % j)
             nc.vector.scalar_tensor_tensor(y[:], b_acc[:], wb_col[:], a_term[:, cols], MULT, ADD)
-            (nc.scalar if j == 1 else nc.sync).dma_start(out[:, cols], y[:])
+            (nc.scalar if j % 2 else nc.sync).dma_start(out[:, cols], y[:])

@@ -24,7 +24,7 @@ F_PASSES = D // (P * PACK)
 LIST_ROWS = 16
 HALF = I // 2
 F_ROWS_FROM = P - QUADRANT
-C_ROWS_FROM, C_ROWS_STEP = 4, 8
+C_ROWS_FROM = P - 16
 PIECES = ((0, HALF), (HALF, HALF // 2), (HALF + HALF // 2, HALF // 2))
 
 
@@ -50,8 +50,8 @@ def tile_attend_noisychannel_kernel(tc, hf, hc, vf_words, vf_scales, vc_words, v
         hc_raw = sb.tile([P, PACK, Q], F32, name="hc_raw", tag="hc_raw", align_bytes=64)
         f_planes = sb.tile([P, F_PASSES * I], U8, name="f_planes", align_bytes=64)
 
-        nc.vector.memset(c_scale_table[:].bitcast(I32), 0)
         nc.vector.memset(f_scale_table[0:F_ROWS_FROM, :].bitcast(I32), 0)
+        nc.vector.memset(c_scale_table[0:C_ROWS_FROM, :].bitcast(I32), 0)
 
         la_col = sb.tile([P, 1], F32, name="la_col")
         lb_col = sb.tile([P, 1], F32, name="lb_col")
@@ -60,15 +60,15 @@ def tile_attend_noisychannel_kernel(tc, hf, hc, vf_words, vf_scales, vc_words, v
         nc.sync.dma_start(f_list[:], offs)
         nc.scalar.dma_start(f_scale_table[F_ROWS_FROM:P, :].bitcast(I32), vf_scales.rearrange("z f c -> f z c").bitcast(I32))
         nc.sync.dma_start(f_tables[0][:].bitcast(I32), vf_words[0].bitcast(I32))
+        nc.scalar.dma_start(c_scale_table[C_ROWS_FROM:P, :].bitcast(I32), vc_scales[0].bitcast(I32))
         nc.sync.dma_start(c_list[:], offs2)
-        nc.sync.dma_start(wa_col[:], wa)
-        nc.sync.dma_start(la_col[:], la)
-        nc.sync.dma_start(lb_col[:], lb)
         nc.sync.dma_start(hf_raw[:], hf.rearrange("(z p t) q -> p z t q", z=F_PASSES, t=PACK))
         nc.sync.dma_start(f_tables[1][:].bitcast(I32), vf_words[1].bitcast(I32))
         nc.sync.dma_start(hc_raw[:], hc.rearrange("(p t) q -> p t q", t=PACK))
-        nc.scalar.dma_start(c_scale_table[C_ROWS_FROM:P:C_ROWS_STEP, :].bitcast(I32), vc_scales[0].bitcast(I32))
         nc.gpsimd.dma_start(wb_col[:], wb)
+        nc.gpsimd.dma_start(lb_col[:], lb)
+        nc.gpsimd.dma_start(wa_col[:], wa)
+        nc.gpsimd.dma_start(la_col[:], la)
 
         f_scale_rows = sb.tile([P, I], U8, name="f_scale_rows", align_bytes=64)
         nc.vector.tensor_copy(f_scale_rows[:], f_scale_table[:].indirect(f_list[:]))
@@ -83,9 +83,9 @@ def tile_attend_noisychannel_kernel(tc, hf, hc, vf_words, vf_scales, vc_words, v
         nc.sync.dma_start(c_table[:].bitcast(I32), vc_words[0].rearrange("p c t -> p (c t)").bitcast(I32))
 
         f_words = [sb.tile([P, I], U16, name="f_words%d" % z, align_bytes=64) for z in range(F_PASSES)]
-        nc.vector.tensor_copy(f_words[0][:], f_tables[0][:].indirect(f_list[:]))
-        c_scale_rows = sb.tile([P, I], U8, name="c_scale_rows", tag="f_table0", align_bytes=64)
+        c_scale_rows = sb.tile([P, I], U8, name="c_scale_rows", align_bytes=64)
         nc.vector.tensor_copy(c_scale_rows[:], c_scale_table[:].indirect(c_list[:]))
+        nc.vector.tensor_copy(f_words[0][:], f_tables[0][:].indirect(f_list[:]))
         nc.vector.tensor_copy(f_words[1][:], f_tables[1][:].indirect(f_list[:]))
 
         hf_grouped = sb.tile([P, F_PASSES, Q, PACK], BF16, name="hf_grouped", align_bytes=64)
@@ -93,10 +93,10 @@ def tile_attend_noisychannel_kernel(tc, hf, hc, vf_words, vf_scales, vc_words, v
         for z in range(F_PASSES):
             cast_and_interleave(nc, hf_grouped[:, z], hf_raw[:, z])
         c_plane = sb.tile([P, I], U8, name="c_plane", tag="hf_raw", align_bytes=64)
-        for r in range(4):
+        for g in (0, 2, 1, 3):
             nc.scalar.dma_start(
-                c_plane[r:P:QUADRANT, :].bitcast(I32),
-                c_scale_rows[C_ROWS_FROM + C_ROWS_STEP * r : P : QUADRANT, :].bitcast(I32),
+                c_plane[QUADRANT * g : QUADRANT * g + 4, :].bitcast(I32),
+                c_scale_rows[C_ROWS_FROM + 4 * g : C_ROWS_FROM + 4 * g + 4, :].bitcast(I32),
             )
         cast_and_interleave(nc, hc_grouped[:], hc_raw[:])
         hf_codes = sb.tile([P, F_PASSES * Q], U32, name="hf_codes", align_bytes=64)

@@ -23,8 +23,11 @@ QUADRANT = 32
 F_PASSES = D // (P * PACK)
 LIST_ROWS = 16
 HALF = I // 2
-F_ROWS_FROM = P - QUADRANT
-C_ROWS_FROM = P - 16
+BLOCKS = 16
+F_ROWS_FROM = P - F_PASSES * BLOCKS
+C_ROWS_FROM = P - BLOCKS
+PLANE_ROWS = 4
+MOVE_ORDER = (0, 2, 1, 3)
 PIECES = ((0, HALF), (HALF, HALF // 2), (HALF + HALF // 2, HALF // 2))
 
 
@@ -45,7 +48,7 @@ def tile_attend_noisychannel_kernel(tc, hf, hc, vf_words, vf_scales, vc_words, v
         c_list = sb.tile([P, I // LIST_ROWS], U16, name="c_list")
         f_scale_table = sb.tile([P, T], U8, name="f_scale_table", tag="f_scale_table", align_bytes=64)
         c_scale_table = sb.tile([P, T], U8, name="c_scale_table", align_bytes=64)
-        f_tables = [sb.tile([P, T], U16, name="f_table%d" % z, tag="f_table%d" % z, align_bytes=64) for z in range(F_PASSES)]
+        f_tables = [sb.tile([P, T], U16, name="f_table%d" % z, align_bytes=64) for z in range(F_PASSES)]
         hf_raw = sb.tile([P, F_PASSES, PACK, Q], F32, name="hf_raw", tag="hf_raw", align_bytes=64)
         hc_raw = sb.tile([P, PACK, Q], F32, name="hc_raw", tag="hc_raw", align_bytes=64)
         f_planes = sb.tile([P, F_PASSES * I], U8, name="f_planes", align_bytes=64)
@@ -53,30 +56,30 @@ def tile_attend_noisychannel_kernel(tc, hf, hc, vf_words, vf_scales, vc_words, v
         nc.vector.memset(f_scale_table[0:F_ROWS_FROM, :].bitcast(I32), 0)
         nc.vector.memset(c_scale_table[0:C_ROWS_FROM, :].bitcast(I32), 0)
 
-        la_col = sb.tile([P, 1], F32, name="la_col")
-        lb_col = sb.tile([P, 1], F32, name="lb_col")
-        wa_col = sb.tile([P, 1], F32, name="wa_col")
-        wb_col = sb.tile([P, 1], F32, name="wb_col")
+        runs = sb.tile([P, QUADRANT], F32, name="runs", align_bytes=64)
+        nc.gpsimd.memset(runs[:], 0.0)
+        run_rows = [vector.rearrange("(g i) o -> g (i o)", i=QUADRANT) for vector in (wa, wb, la, lb)]
+
         nc.sync.dma_start(f_list[:], offs)
         nc.scalar.dma_start(f_scale_table[F_ROWS_FROM:P, :].bitcast(I32), vf_scales.rearrange("z f c -> f z c").bitcast(I32))
         nc.sync.dma_start(f_tables[0][:].bitcast(I32), vf_words[0].bitcast(I32))
         nc.scalar.dma_start(c_scale_table[C_ROWS_FROM:P, :].bitcast(I32), vc_scales[0].bitcast(I32))
         nc.sync.dma_start(c_list[:], offs2)
+        for j in (0, 1):
+            nc.sync.dma_start(runs[j:P:QUADRANT, :], run_rows[j])
         nc.sync.dma_start(hf_raw[:], hf.rearrange("(z p t) q -> p z t q", z=F_PASSES, t=PACK))
         nc.sync.dma_start(f_tables[1][:].bitcast(I32), vf_words[1].bitcast(I32))
         nc.sync.dma_start(hc_raw[:], hc.rearrange("(p t) q -> p t q", t=PACK))
-        nc.gpsimd.dma_start(wb_col[:], wb)
-        nc.gpsimd.dma_start(lb_col[:], lb)
-        nc.gpsimd.dma_start(wa_col[:], wa)
-        nc.gpsimd.dma_start(la_col[:], la)
+        for j in (2, 3):
+            nc.gpsimd.dma_start(runs[j:P:QUADRANT, :], run_rows[j])
 
         f_scale_rows = sb.tile([P, I], U8, name="f_scale_rows", align_bytes=64)
         nc.vector.tensor_copy(f_scale_rows[:], f_scale_table[:].indirect(f_list[:]))
-        rows_a_move = PACK * F_PASSES
-        for g in (0, 2, 1, 3):
+        rows_a_move = PLANE_ROWS * F_PASSES
+        for g in MOVE_ORDER:
             first = F_ROWS_FROM + rows_a_move * g
             nc.sync.dma_start(
-                f_planes[QUADRANT * g : QUADRANT * g + 4, :].bitcast(I32),
+                f_planes[QUADRANT * g : QUADRANT * g + PLANE_ROWS, :].bitcast(I32),
                 f_scale_rows[first : first + rows_a_move, :].bitcast(I32),
             )
         c_table = sb.tile([P, T], U32, name="c_table", tag="f_scale_table", align_bytes=64)
@@ -85,18 +88,19 @@ def tile_attend_noisychannel_kernel(tc, hf, hc, vf_words, vf_scales, vc_words, v
         f_words = [sb.tile([P, I], U16, name="f_words%d" % z, align_bytes=64) for z in range(F_PASSES)]
         c_scale_rows = sb.tile([P, I], U8, name="c_scale_rows", align_bytes=64)
         nc.vector.tensor_copy(c_scale_rows[:], c_scale_table[:].indirect(c_list[:]))
-        nc.vector.tensor_copy(f_words[0][:], f_tables[0][:].indirect(f_list[:]))
-        nc.vector.tensor_copy(f_words[1][:], f_tables[1][:].indirect(f_list[:]))
+        for z in range(F_PASSES):
+            nc.vector.tensor_copy(f_words[z][:], f_tables[z][:].indirect(f_list[:]))
 
-        hf_grouped = sb.tile([P, F_PASSES, Q, PACK], BF16, name="hf_grouped", align_bytes=64)
+        hf_grouped = sb.tile([P, F_PASSES, Q, PACK], BF16, name="hf_grouped", tag="hf_grouped", align_bytes=64)
         hc_grouped = sb.tile([P, Q, PACK], BF16, name="hc_grouped", align_bytes=64)
         for z in range(F_PASSES):
             cast_and_interleave(nc, hf_grouped[:, z], hf_raw[:, z])
         c_plane = sb.tile([P, I], U8, name="c_plane", tag="hf_raw", align_bytes=64)
-        for g in (0, 2, 1, 3):
+        for g in MOVE_ORDER:
+            first = C_ROWS_FROM + PLANE_ROWS * g
             nc.scalar.dma_start(
-                c_plane[QUADRANT * g : QUADRANT * g + 4, :].bitcast(I32),
-                c_scale_rows[C_ROWS_FROM + 4 * g : C_ROWS_FROM + 4 * g + 4, :].bitcast(I32),
+                c_plane[QUADRANT * g : QUADRANT * g + PLANE_ROWS, :].bitcast(I32),
+                c_scale_rows[first : first + PLANE_ROWS, :].bitcast(I32),
             )
         cast_and_interleave(nc, hc_grouped[:], hc_raw[:])
         hf_codes = sb.tile([P, F_PASSES * Q], U32, name="hf_codes", align_bytes=64)
@@ -118,14 +122,17 @@ def tile_attend_noisychannel_kernel(tc, hf, hc, vf_words, vf_scales, vc_words, v
                 stop=(z == F_PASSES - 1),
             )
 
+        vector_cols = sb.tile([P, QUADRANT], F32, name="vector_cols", tag="hf_grouped", align_bytes=64)
+        nc.vector.transpose(vector_cols[:], runs[:])
+        wa_col, wb_col, la_col, lb_col = (vector_cols[:, j : j + 1] for j in range(len(run_rows)))
         wb_lb = sb.tile([P, 1], F32, name="wb_lb", tag="hc_raw", align_bytes=64)
         weighted_sums = sb.tile([P, 1], F32, name="weighted_sums")
         bias_col = sb.tile([P, 1], F32, name="bias_col")
-        nc.scalar.activation(wb_lb[:], lb_col[:], IDENTITY, scale=wb_col[:])
-        nc.scalar.activation(weighted_sums[:], la_col[:], IDENTITY, bias=wb_lb[:], scale=wa_col[:])
+        nc.scalar.activation(wb_lb[:], lb_col, IDENTITY, scale=wb_col)
+        nc.scalar.activation(weighted_sums[:], la_col, IDENTITY, bias=wb_lb[:], scale=wa_col)
         nc.scalar.activation(bias_col[:], weighted_sums[:], IDENTITY, scale=-1.0)
         a_term = sb.tile([P, I], F32, name="a_term")
-        nc.scalar.activation(a_term[:], a_acc[:], IDENTITY, bias=bias_col[:], scale=wa_col[:])
+        nc.scalar.activation(a_term[:], a_acc[:], IDENTITY, bias=bias_col[:], scale=wa_col)
 
         c_words = [sb.tile([P, HALF], U32, name="c_words%d" % h, align_bytes=64) for h in range(2)]
         for h in range(2):
@@ -144,5 +151,5 @@ def tile_attend_noisychannel_kernel(tc, hf, hc, vf_words, vf_scales, vc_words, v
                 stop=True,
             )
             y = sb.tile([P, width], F32, name="y%d" % j)
-            nc.vector.scalar_tensor_tensor(y[:], b_acc[:], wb_col[:], a_term[:, cols], MULT, ADD)
+            nc.vector.scalar_tensor_tensor(y[:], b_acc[:], wb_col, a_term[:, cols], MULT, ADD)
             (nc.scalar if j % 2 else nc.sync).dma_start(out[:, cols], y[:])

@@ -49,7 +49,7 @@ def tile_attend_noisychannel_kernel(tc, hf, hc, vf_words, vf_scales, vc_words, v
         f_scale_table = sb.tile([P, T], U8, name="f_scale_table", tag="f_scale_table", align_bytes=64)
         c_scale_table = sb.tile([P, T], U8, name="c_scale_table", align_bytes=64)
         f_tables = [sb.tile([P, T], U16, name="f_table%d" % z, align_bytes=64) for z in range(F_PASSES)]
-        hf_raw = sb.tile([P, F_PASSES, PACK, Q], F32, name="hf_raw", tag="hf_raw", align_bytes=64)
+        hf_raw = sb.tile([P, F_PASSES, PACK, Q], F32, name="hf_raw", align_bytes=64)
         hc_raw = sb.tile([P, PACK, Q], F32, name="hc_raw", tag="hc_raw", align_bytes=64)
         f_planes = sb.tile([P, F_PASSES * I], U8, name="f_planes", align_bytes=64)
 
@@ -95,10 +95,10 @@ def tile_attend_noisychannel_kernel(tc, hf, hc, vf_words, vf_scales, vc_words, v
         hc_grouped = sb.tile([P, Q, PACK], BF16, name="hc_grouped", align_bytes=64)
         for z in range(F_PASSES):
             cast_and_interleave(nc, hf_grouped[:, z], hf_raw[:, z])
-        c_plane = sb.tile([P, I], U8, name="c_plane", tag="hf_raw", align_bytes=64)
+        c_plane = sb.tile([P, I], U8, name="c_plane", align_bytes=64)
         for g in MOVE_ORDER:
             first = C_ROWS_FROM + PLANE_ROWS * g
-            nc.scalar.dma_start(
+            nc.sync.dma_start(
                 c_plane[QUADRANT * g : QUADRANT * g + PLANE_ROWS, :].bitcast(I32),
                 c_scale_rows[first : first + PLANE_ROWS, :].bitcast(I32),
             )

@@ -18,6 +18,7 @@ ADD = mybir.AluOpType.add
 IDENTITY = mybir.ActivationFunctionType.Identity
 
 P = 128
+DMA_ALIGN = 256
 PACK = 4
 QUADRANT = 32
 F_PASSES = D // (P * PACK)
@@ -44,19 +45,19 @@ def tile_attend_noisychannel_kernel(tc, hf, hc, vf_words, vf_scales, vc_words, v
         sb = ctx.enter_context(tc.tile_pool(name="sb", bufs=1))
         psum = ctx.enter_context(tc.psum_pool(name="psum", bufs=1))
 
-        f_list = sb.tile([P, I // LIST_ROWS], U16, name="f_list")
-        c_list = sb.tile([P, I // LIST_ROWS], U16, name="c_list")
-        f_scale_table = sb.tile([P, T], U8, name="f_scale_table", tag="f_scale_table", align_bytes=64)
-        c_scale_table = sb.tile([P, T], U8, name="c_scale_table", align_bytes=64)
-        f_tables = [sb.tile([P, T], U16, name="f_table%d" % z, align_bytes=64) for z in range(F_PASSES)]
-        hf_raw = sb.tile([P, F_PASSES, PACK, Q], F32, name="hf_raw", align_bytes=64)
-        hc_raw = sb.tile([P, PACK, Q], F32, name="hc_raw", tag="hc_raw", align_bytes=64)
-        f_planes = sb.tile([P, F_PASSES * I], U8, name="f_planes", align_bytes=64)
+        f_list = sb.tile([P, I // LIST_ROWS], U16, name="f_list", align_bytes=DMA_ALIGN)
+        c_list = sb.tile([P, I // LIST_ROWS], U16, name="c_list", align_bytes=DMA_ALIGN)
+        f_scale_table = sb.tile([P, T], U8, name="f_scale_table", tag="f_scale_table", align_bytes=DMA_ALIGN)
+        c_scale_table = sb.tile([P, T], U8, name="c_scale_table", align_bytes=DMA_ALIGN)
+        f_tables = [sb.tile([P, T], U16, name="f_table%d" % z, align_bytes=DMA_ALIGN) for z in range(F_PASSES)]
+        hf_raw = sb.tile([P, F_PASSES, PACK, Q], F32, name="hf_raw", align_bytes=DMA_ALIGN)
+        hc_raw = sb.tile([P, PACK, Q], F32, name="hc_raw", tag="hc_raw", align_bytes=DMA_ALIGN)
+        f_planes = sb.tile([P, F_PASSES * I], U8, name="f_planes", align_bytes=DMA_ALIGN)
 
         nc.vector.memset(f_scale_table[0:F_ROWS_FROM, :].bitcast(I32), 0)
         nc.vector.memset(c_scale_table[0:C_ROWS_FROM, :].bitcast(I32), 0)
 
-        runs = sb.tile([P, QUADRANT], F32, name="runs", align_bytes=64)
+        runs = sb.tile([P, QUADRANT], F32, name="runs", align_bytes=DMA_ALIGN)
         nc.gpsimd.memset(runs[:], 0.0)
         run_rows = [vector.rearrange("(g i) o -> g (i o)", i=QUADRANT) for vector in (wa, wb, la, lb)]
 
@@ -73,7 +74,7 @@ def tile_attend_noisychannel_kernel(tc, hf, hc, vf_words, vf_scales, vc_words, v
         for j in (2, 3):
             nc.gpsimd.dma_start(runs[j:P:QUADRANT, :], run_rows[j])
 
-        f_scale_rows = sb.tile([P, I], U8, name="f_scale_rows", align_bytes=64)
+        f_scale_rows = sb.tile([P, I], U8, name="f_scale_rows", align_bytes=DMA_ALIGN)
         nc.vector.tensor_copy(f_scale_rows[:], f_scale_table[:].indirect(f_list[:]))
         rows_a_move = PLANE_ROWS * F_PASSES
         for g in MOVE_ORDER:
@@ -82,11 +83,11 @@ def tile_attend_noisychannel_kernel(tc, hf, hc, vf_words, vf_scales, vc_words, v
                 f_planes[QUADRANT * g : QUADRANT * g + PLANE_ROWS, :].bitcast(I32),
                 f_scale_rows[first : first + rows_a_move, :].bitcast(I32),
             )
-        c_table = sb.tile([P, T], U32, name="c_table", tag="f_scale_table", align_bytes=64)
+        c_table = sb.tile([P, T], U32, name="c_table", tag="f_scale_table", align_bytes=DMA_ALIGN)
         nc.sync.dma_start(c_table[:].bitcast(I32), vc_words[0].rearrange("p c t -> p (c t)").bitcast(I32))
 
         f_words = [sb.tile([P, I], U16, name="f_words%d" % z, align_bytes=64) for z in range(F_PASSES)]
-        c_scale_rows = sb.tile([P, I], U8, name="c_scale_rows", align_bytes=64)
+        c_scale_rows = sb.tile([P, I], U8, name="c_scale_rows", align_bytes=DMA_ALIGN)
         nc.vector.tensor_copy(c_scale_rows[:], c_scale_table[:].indirect(c_list[:]))
         for z in range(F_PASSES):
             nc.vector.tensor_copy(f_words[z][:], f_tables[z][:].indirect(f_list[:]))
@@ -95,7 +96,7 @@ def tile_attend_noisychannel_kernel(tc, hf, hc, vf_words, vf_scales, vc_words, v
         hc_grouped = sb.tile([P, Q, PACK], BF16, name="hc_grouped", align_bytes=64)
         for z in range(F_PASSES):
             cast_and_interleave(nc, hf_grouped[:, z], hf_raw[:, z])
-        c_plane = sb.tile([P, I], U8, name="c_plane", align_bytes=64)
+        c_plane = sb.tile([P, I], U8, name="c_plane", align_bytes=DMA_ALIGN)
         for g in MOVE_ORDER:
             first = C_ROWS_FROM + PLANE_ROWS * g
             nc.sync.dma_start(
@@ -125,7 +126,7 @@ def tile_attend_noisychannel_kernel(tc, hf, hc, vf_words, vf_scales, vc_words, v
         vector_cols = sb.tile([P, QUADRANT], F32, name="vector_cols", tag="hf_grouped", align_bytes=64)
         nc.vector.transpose(vector_cols[:], runs[:])
         wa_col, wb_col, la_col, lb_col = (vector_cols[:, j : j + 1] for j in range(len(run_rows)))
-        wb_lb = sb.tile([P, 1], F32, name="wb_lb", tag="hc_raw", align_bytes=64)
+        wb_lb = sb.tile([P, 1], F32, name="wb_lb", tag="hc_raw", align_bytes=DMA_ALIGN)
         weighted_sums = sb.tile([P, 1], F32, name="weighted_sums")
         bias_col = sb.tile([P, 1], F32, name="bias_col")
         nc.scalar.activation(wb_lb[:], lb_col, IDENTITY, scale=wb_col)
@@ -150,6 +151,6 @@ def tile_attend_noisychannel_kernel(tc, hf, hc, vf_words, vf_scales, vc_words, v
                 start=True,
                 stop=True,
             )
-            y = sb.tile([P, width], F32, name="y%d" % j)
+            y = sb.tile([P, width], F32, name="y%d" % j, align_bytes=DMA_ALIGN)
             nc.vector.scalar_tensor_tensor(y[:], b_acc[:], wb_col, a_term[:, cols], MULT, ADD)
             (nc.scalar if j % 2 else nc.sync).dma_start(out[:, cols], y[:])

@@ -18,7 +18,7 @@ ADD = mybir.AluOpType.add
 IDENTITY = mybir.ActivationFunctionType.Identity
 
 P = 128
-DMA_ALIGN = 256
+DMA_ALIGN = 2048
 PACK = 4
 QUADRANT = 32
 F_PASSES = D // (P * PACK)
@@ -27,6 +27,7 @@ HALF = I // 2
 BLOCKS = 16
 F_ROWS_FROM = P - F_PASSES * BLOCKS
 C_ROWS_FROM = P - BLOCKS
+C_FIRST = T // 4
 PLANE_ROWS = 4
 MOVE_ORDER = (0, 2, 1, 3)
 PIECES = ((0, HALF), (HALF, HALF // 2), (HALF + HALF // 2, HALF // 2))
@@ -39,27 +40,44 @@ def cast_and_interleave(nc, grouped, raw):
     )
 
 
+def move_rows(queue, plane, rows, first_row, rows_a_move):
+    for g in MOVE_ORDER:
+        first = first_row + rows_a_move * g
+        queue.dma_start(
+            plane[QUADRANT * g : QUADRANT * g + PLANE_ROWS, :].bitcast(I32),
+            rows[first : first + rows_a_move, :].bitcast(I32),
+        )
+
+
 def tile_attend_noisychannel_kernel(tc, hf, hc, vf_words, vf_scales, vc_words, vc_scales, la, lb, wa, wb, offs, offs2, out):
     nc = tc.nc
     with ExitStack() as ctx:
+        moved = ctx.enter_context(tc.tile_pool(name="moved", bufs=1))
         sb = ctx.enter_context(tc.tile_pool(name="sb", bufs=1))
         psum = ctx.enter_context(tc.psum_pool(name="psum", bufs=1))
 
-        f_list = sb.tile([P, I // LIST_ROWS], U16, name="f_list", align_bytes=DMA_ALIGN)
-        c_list = sb.tile([P, I // LIST_ROWS], U16, name="c_list", align_bytes=DMA_ALIGN)
-        f_scale_table = sb.tile([P, T], U8, name="f_scale_table", tag="f_scale_table", align_bytes=DMA_ALIGN)
-        c_scale_table = sb.tile([P, T], U8, name="c_scale_table", align_bytes=DMA_ALIGN)
-        f_tables = [sb.tile([P, T], U16, name="f_table%d" % z, align_bytes=DMA_ALIGN) for z in range(F_PASSES)]
-        hf_raw = sb.tile([P, F_PASSES, PACK, Q], F32, name="hf_raw", align_bytes=DMA_ALIGN)
-        hc_raw = sb.tile([P, PACK, Q], F32, name="hc_raw", tag="hc_raw", align_bytes=DMA_ALIGN)
-        f_planes = sb.tile([P, F_PASSES * I], U8, name="f_planes", align_bytes=DMA_ALIGN)
+        def dma_tile(shape, dtype, name):
+            return moved.tile(shape, dtype, name=name, tag=name, align_bytes=DMA_ALIGN)
+
+        f_list = dma_tile([P, I // LIST_ROWS], U16, "f_list")
+        c_list = dma_tile([P, I // LIST_ROWS], U16, "c_list")
+        f_scale_table = dma_tile([P, T], U8, "f_scale_table")
+        c_scale_table = dma_tile([P, T], U8, "c_scale_table")
+        f_tables = [dma_tile([P, T], U16, "f_table%d" % z) for z in range(F_PASSES)]
+        c_table = dma_tile([P, T], U32, "c_table")
+        hf_raw = dma_tile([P, F_PASSES, PACK, Q], F32, "hf_raw")
+        hc_raw = dma_tile([P, PACK, Q], F32, "hc_raw")
+        f_scale_rows = dma_tile([P, I], U8, "f_scale_rows")
+        c_scale_rows = dma_tile([P, I], U8, "c_scale_rows")
+        f_planes = dma_tile([P, F_PASSES * I], U8, "f_planes")
+        c_plane = dma_tile([P, I], U8, "c_plane")
+        runs = dma_tile([P, QUADRANT], F32, "runs")
 
         nc.vector.memset(f_scale_table[0:F_ROWS_FROM, :].bitcast(I32), 0)
         nc.vector.memset(c_scale_table[0:C_ROWS_FROM, :].bitcast(I32), 0)
-
-        runs = sb.tile([P, QUADRANT], F32, name="runs", align_bytes=DMA_ALIGN)
         nc.gpsimd.memset(runs[:], 0.0)
         run_rows = [vector.rearrange("(g i) o -> g (i o)", i=QUADRANT) for vector in (wa, wb, la, lb)]
+        c_words_in = vc_words[0].rearrange("p c t -> p (c t)").bitcast(I32)
 
         nc.sync.dma_start(f_list[:], offs)
         nc.scalar.dma_start(f_scale_table[F_ROWS_FROM:P, :].bitcast(I32), vf_scales.rearrange("z f c -> f z c").bitcast(I32))
@@ -71,24 +89,16 @@ def tile_attend_noisychannel_kernel(tc, hf, hc, vf_words, vf_scales, vc_words, v
         nc.sync.dma_start(hf_raw[:], hf.rearrange("(z p t) q -> p z t q", z=F_PASSES, t=PACK))
         nc.sync.dma_start(f_tables[1][:].bitcast(I32), vf_words[1].bitcast(I32))
         nc.sync.dma_start(hc_raw[:], hc.rearrange("(p t) q -> p t q", t=PACK))
+        nc.sync.dma_start(c_table[:, 0:C_FIRST].bitcast(I32), c_words_in[:, 0:C_FIRST])
         for j in (2, 3):
             nc.gpsimd.dma_start(runs[j:P:QUADRANT, :], run_rows[j])
 
-        f_scale_rows = sb.tile([P, I], U8, name="f_scale_rows", align_bytes=DMA_ALIGN)
         nc.vector.tensor_copy(f_scale_rows[:], f_scale_table[:].indirect(f_list[:]))
-        rows_a_move = PLANE_ROWS * F_PASSES
-        for g in MOVE_ORDER:
-            first = F_ROWS_FROM + rows_a_move * g
-            nc.sync.dma_start(
-                f_planes[QUADRANT * g : QUADRANT * g + PLANE_ROWS, :].bitcast(I32),
-                f_scale_rows[first : first + rows_a_move, :].bitcast(I32),
-            )
-        c_table = sb.tile([P, T], U32, name="c_table", tag="f_scale_table", align_bytes=DMA_ALIGN)
-        nc.sync.dma_start(c_table[:].bitcast(I32), vc_words[0].rearrange("p c t -> p (c t)").bitcast(I32))
-
-        f_words = [sb.tile([P, I], U16, name="f_words%d" % z, align_bytes=64) for z in range(F_PASSES)]
-        c_scale_rows = sb.tile([P, I], U8, name="c_scale_rows", align_bytes=DMA_ALIGN)
+        move_rows(nc.sync, f_planes, f_scale_rows, F_ROWS_FROM, PLANE_ROWS * F_PASSES)
+        nc.sync.dma_start(c_table[:, C_FIRST:T].bitcast(I32), c_words_in[:, C_FIRST:T])
         nc.vector.tensor_copy(c_scale_rows[:], c_scale_table[:].indirect(c_list[:]))
+        move_rows(nc.sync, c_plane, c_scale_rows, C_ROWS_FROM, PLANE_ROWS)
+        f_words = [sb.tile([P, I], U16, name="f_words%d" % z, align_bytes=64) for z in range(F_PASSES)]
         for z in range(F_PASSES):
             nc.vector.tensor_copy(f_words[z][:], f_tables[z][:].indirect(f_list[:]))
 
@@ -96,13 +106,6 @@ def tile_attend_noisychannel_kernel(tc, hf, hc, vf_words, vf_scales, vc_words, v
         hc_grouped = sb.tile([P, Q, PACK], BF16, name="hc_grouped", align_bytes=64)
         for z in range(F_PASSES):
             cast_and_interleave(nc, hf_grouped[:, z], hf_raw[:, z])
-        c_plane = sb.tile([P, I], U8, name="c_plane", align_bytes=DMA_ALIGN)
-        for g in MOVE_ORDER:
-            first = C_ROWS_FROM + PLANE_ROWS * g
-            nc.sync.dma_start(
-                c_plane[QUADRANT * g : QUADRANT * g + PLANE_ROWS, :].bitcast(I32),
-                c_scale_rows[first : first + PLANE_ROWS, :].bitcast(I32),
-            )
         cast_and_interleave(nc, hc_grouped[:], hc_raw[:])
         hf_codes = sb.tile([P, F_PASSES * Q], U32, name="hf_codes", align_bytes=64)
         hf_plane = sb.tile([P, F_PASSES * Q], U8, name="hf_plane", align_bytes=64)
@@ -126,7 +129,7 @@ def tile_attend_noisychannel_kernel(tc, hf, hc, vf_words, vf_scales, vc_words, v
         vector_cols = sb.tile([P, QUADRANT], F32, name="vector_cols", tag="hf_grouped", align_bytes=64)
         nc.vector.transpose(vector_cols[:], runs[:])
         wa_col, wb_col, la_col, lb_col = (vector_cols[:, j : j + 1] for j in range(len(run_rows)))
-        wb_lb = sb.tile([P, 1], F32, name="wb_lb", tag="hc_raw", align_bytes=DMA_ALIGN)
+        wb_lb = moved.tile([P, 1], F32, name="wb_lb", tag="hc_raw", align_bytes=DMA_ALIGN)
         weighted_sums = sb.tile([P, 1], F32, name="weighted_sums")
         bias_col = sb.tile([P, 1], F32, name="bias_col")
         nc.scalar.activation(wb_lb[:], lb_col, IDENTITY, scale=wb_col)
@@ -151,6 +154,6 @@ def tile_attend_noisychannel_kernel(tc, hf, hc, vf_words, vf_scales, vc_words, v
                 start=True,
                 stop=True,
             )
-            y = sb.tile([P, width], F32, name="y%d" % j, align_bytes=DMA_ALIGN)
+            y = dma_tile([P, width], F32, "y%d" % j)
             nc.vector.scalar_tensor_tensor(y[:], b_acc[:], wb_col, a_term[:, cols], MULT, ADD)
             (nc.scalar if j % 2 else nc.sync).dma_start(out[:, cols], y[:])

@@ -116,15 +116,26 @@ def tile_attend_noisychannel_kernel(tc, hf, hc, vf_words, vf_scales, vc_words, v
 
         a_acc = psum.tile([P, I], F32, name="a_acc")
         for z in range(F_PASSES):
-            nc.tensor.matmul_mx(
-                out=a_acc[:],
-                lhsT=hf_codes[:, z * Q : (z + 1) * Q].bitcast(FP8X4),
-                lhsT_scale=hf_plane[:, z * Q : (z + 1) * Q],
-                rhs=f_words[z][:].bitcast(FP4X4),
-                rhs_scale=f_planes[:, z * I : (z + 1) * I],
-                start=(z == 0),
-                stop=(z == F_PASSES - 1),
-            )
+            for first in range(0, I, Q):
+                nc.tensor.matmul_mx(
+                    out=a_acc[:, first : first + Q],
+                    lhsT=hf_codes[:, z * Q : (z + 1) * Q].bitcast(FP8X4),
+                    lhsT_scale=hf_plane[:, z * Q : (z + 1) * Q],
+                    rhs=f_words[z][:, first : first + Q].bitcast(FP4X4),
+                    rhs_scale=f_planes[:, z * I + first : z * I + first + Q],
+                    start=(z == 0 and first == 0),
+                    stop=(z == F_PASSES - 1 and first == I - Q),
+                )
+        warm_acc = psum.tile([P, HALF], F32, name="warm_acc")
+        nc.tensor.matmul_mx(
+            out=warm_acc[:],
+            lhsT=hf_codes[:, Q : 2 * Q].bitcast(FP8X4),
+            lhsT_scale=hf_plane[:, Q : 2 * Q],
+            rhs=f_words[1][:, 0:HALF].bitcast(FP4X4),
+            rhs_scale=f_planes[:, I : I + HALF],
+            start=True,
+            stop=True,
+        )
 
         vector_cols = sb.tile([P, QUADRANT], F32, name="vector_cols", tag="hf_grouped", align_bytes=64)
         nc.vector.transpose(vector_cols[:], runs[:])

@@ -87,17 +87,18 @@ def tile_attend_noisychannel_kernel(tc, hf, hc, vf_words, vf_scales, vc_words, v
         for j in (0, 1):
             nc.sync.dma_start(runs[j:P:QUADRANT, :], run_rows[j])
         nc.sync.dma_start(hf_raw[:], hf.rearrange("(z p t) q -> p z t q", z=F_PASSES, t=PACK))
+        nc.sync.dma_start(runs[2:P:QUADRANT, :], run_rows[2])
         nc.sync.dma_start(f_tables[1][:].bitcast(I32), vf_words[1].bitcast(I32))
         nc.sync.dma_start(hc_raw[:], hc.rearrange("(p t) q -> p t q", t=PACK))
         nc.sync.dma_start(c_table[:, 0:C_FIRST].bitcast(I32), c_words_in[:, 0:C_FIRST])
-        for j in (2, 3):
-            nc.gpsimd.dma_start(runs[j:P:QUADRANT, :], run_rows[j])
+        nc.gpsimd.dma_start(runs[3:P:QUADRANT, :], run_rows[3])
 
         nc.vector.tensor_copy(f_scale_rows[:], f_scale_table[:].indirect(f_list[:]))
         move_rows(nc.sync, f_planes, f_scale_rows, F_ROWS_FROM, PLANE_ROWS * F_PASSES)
         nc.sync.dma_start(c_table[:, C_FIRST:T].bitcast(I32), c_words_in[:, C_FIRST:T])
         nc.vector.tensor_copy(c_scale_rows[:], c_scale_table[:].indirect(c_list[:]))
-        move_rows(nc.sync, c_plane, c_scale_rows, C_ROWS_FROM, PLANE_ROWS)
+        for r in range(PLANE_ROWS):
+            nc.sync.dma_start(c_plane[r:P:QUADRANT, :].bitcast(I32), c_scale_rows[C_ROWS_FROM + r : P : PLANE_ROWS, :].bitcast(I32))
         f_words = [sb.tile([P, I], U16, name="f_words%d" % z, align_bytes=64) for z in range(F_PASSES)]
         for z in range(F_PASSES):
             nc.vector.tensor_copy(f_words[z][:], f_tables[z][:].indirect(f_list[:]))

@@ -73,9 +73,9 @@ def tile_attend_noisychannel_kernel(tc, hf, hc, vf_words, vf_scales, vc_words, v
         c_plane = dma_tile([P, I], U8, "c_plane")
         runs = dma_tile([P, QUADRANT], F32, "runs")
 
+        nc.vector.memset(runs[:], 0.0)
         nc.vector.memset(f_scale_table[0:F_ROWS_FROM, :].bitcast(I32), 0)
         nc.vector.memset(c_scale_table[0:C_ROWS_FROM, :].bitcast(I32), 0)
-        nc.gpsimd.memset(runs[:], 0.0)
         run_rows = [vector.rearrange("(g i) o -> g (i o)", i=QUADRANT) for vector in (wa, wb, la, lb)]
         c_words_in = vc_words[0].rearrange("p c t -> p (c t)").bitcast(I32)
 

@@ -26,10 +26,11 @@ LIST_ROWS = 16
 HALF = I // 2
 BLOCKS = 16
 F_ROWS_FROM = P - F_PASSES * BLOCKS
-C_ROWS_FROM = P - BLOCKS
+C_ROWS_TO = P // 2
+C_ROWS_FROM = C_ROWS_TO - BLOCKS
 C_FIRST = T // 4
 PLANE_ROWS = 4
-MOVE_ORDER = (0, 2, 1, 3)
+QUADRANT_ORDER = (0, 2, 1, 3)
 PIECES = ((0, HALF), (HALF, HALF // 2), (HALF + HALF // 2, HALF // 2))
 
 
@@ -38,15 +39,6 @@ def cast_and_interleave(nc, grouped, raw):
         out=grouped.rearrange("p (c i) t -> p c t i", i=4),
         in_=raw.rearrange("p t (c i) -> p c t i", i=4),
     )
-
-
-def move_rows(queue, plane, rows, first_row, rows_a_move):
-    for g in MOVE_ORDER:
-        first = first_row + rows_a_move * g
-        queue.dma_start(
-            plane[QUADRANT * g : QUADRANT * g + PLANE_ROWS, :].bitcast(I32),
-            rows[first : first + rows_a_move, :].bitcast(I32),
-        )
 
 
 def tile_attend_noisychannel_kernel(tc, hf, hc, vf_words, vf_scales, vc_words, vc_scales, la, lb, wa, wb, offs, offs2, out):
@@ -76,13 +68,14 @@ def tile_attend_noisychannel_kernel(tc, hf, hc, vf_words, vf_scales, vc_words, v
         nc.vector.memset(runs[:], 0.0)
         nc.vector.memset(f_scale_table[0:F_ROWS_FROM, :].bitcast(I32), 0)
         nc.vector.memset(c_scale_table[0:C_ROWS_FROM, :].bitcast(I32), 0)
+        nc.vector.memset(c_scale_table[C_ROWS_TO:P, :].bitcast(I32), 0)
         run_rows = [vector.rearrange("(g i) o -> g (i o)", i=QUADRANT) for vector in (wa, wb, la, lb)]
         c_words_in = vc_words[0].rearrange("p c t -> p (c t)").bitcast(I32)
 
         nc.sync.dma_start(f_list[:], offs)
         nc.scalar.dma_start(f_scale_table[F_ROWS_FROM:P, :].bitcast(I32), vf_scales.rearrange("z f c -> f z c").bitcast(I32))
         nc.sync.dma_start(f_tables[0][:].bitcast(I32), vf_words[0].bitcast(I32))
-        nc.scalar.dma_start(c_scale_table[C_ROWS_FROM:P, :].bitcast(I32), vc_scales[0].bitcast(I32))
+        nc.scalar.dma_start(c_scale_table[C_ROWS_FROM:C_ROWS_TO, :].bitcast(I32), vc_scales[0].bitcast(I32))
         nc.sync.dma_start(c_list[:], offs2)
         for j in (0, 1):
             nc.sync.dma_start(runs[j:P:QUADRANT, :], run_rows[j])
@@ -94,11 +87,19 @@ def tile_attend_noisychannel_kernel(tc, hf, hc, vf_words, vf_scales, vc_words, v
         nc.gpsimd.dma_start(runs[3:P:QUADRANT, :], run_rows[3])
 
         nc.vector.tensor_copy(f_scale_rows[:], f_scale_table[:].indirect(f_list[:]))
-        move_rows(nc.sync, f_planes, f_scale_rows, F_ROWS_FROM, PLANE_ROWS * F_PASSES)
+        for g in QUADRANT_ORDER:
+            first = F_ROWS_FROM + PLANE_ROWS * F_PASSES * g
+            nc.sync.dma_start(
+                f_planes[QUADRANT * g : QUADRANT * g + PLANE_ROWS, :].bitcast(I32),
+                f_scale_rows[first : first + PLANE_ROWS * F_PASSES, :].bitcast(I32),
+            )
         nc.sync.dma_start(c_table[:, C_FIRST:T].bitcast(I32), c_words_in[:, C_FIRST:T])
         nc.vector.tensor_copy(c_scale_rows[:], c_scale_table[:].indirect(c_list[:]))
         for r in range(PLANE_ROWS):
-            nc.sync.dma_start(c_plane[r:P:QUADRANT, :].bitcast(I32), c_scale_rows[C_ROWS_FROM + r : P : PLANE_ROWS, :].bitcast(I32))
+            nc.sync.dma_start(
+                c_plane[r:P:QUADRANT, :].bitcast(I32),
+                c_scale_rows[C_ROWS_FROM + r : C_ROWS_TO : PLANE_ROWS, :].bitcast(I32),
+            )
         f_words = [sb.tile([P, I], U16, name="f_words%d" % z, align_bytes=64) for z in range(F_PASSES)]
         for z in range(F_PASSES):
             nc.vector.tensor_copy(f_words[z][:], f_tables[z][:].indirect(f_list[:]))

@@ -118,26 +118,15 @@ def tile_attend_noisychannel_kernel(tc, hf, hc, vf_words, vf_scales, vc_words, v
 
         a_acc = psum.tile([P, I], F32, name="a_acc")
         for z in range(F_PASSES):
-            for first in range(0, I, Q):
-                nc.tensor.matmul_mx(
-                    out=a_acc[:, first : first + Q],
-                    lhsT=hf_codes[:, z * Q : (z + 1) * Q].bitcast(FP8X4),
-                    lhsT_scale=hf_plane[:, z * Q : (z + 1) * Q],
-                    rhs=f_words[z][:, first : first + Q].bitcast(FP4X4),
-                    rhs_scale=f_planes[:, z * I + first : z * I + first + Q],
-                    start=(z == 0 and first == 0),
-                    stop=(z == F_PASSES - 1 and first == I - Q),
-                )
-        warm_acc = psum.tile([P, HALF], F32, name="warm_acc")
-        nc.tensor.matmul_mx(
-            out=warm_acc[:],
-            lhsT=hf_codes[:, Q : 2 * Q].bitcast(FP8X4),
-            lhsT_scale=hf_plane[:, Q : 2 * Q],
-            rhs=f_words[1][:, 0:HALF].bitcast(FP4X4),
-            rhs_scale=f_planes[:, I : I + HALF],
-            start=True,
-            stop=True,
-        )
+            nc.tensor.matmul_mx(
+                out=a_acc[:],
+                lhsT=hf_codes[:, z * Q : (z + 1) * Q].bitcast(FP8X4),
+                lhsT_scale=hf_plane[:, z * Q : (z + 1) * Q],
+                rhs=f_words[z][:].bitcast(FP4X4),
+                rhs_scale=f_planes[:, z * I : (z + 1) * I],
+                start=(z == 0),
+                stop=(z == F_PASSES - 1),
+            )
 
         vector_cols = sb.tile([P, QUADRANT], F32, name="vector_cols", tag="hf_grouped", align_bytes=64)
         nc.vector.transpose(vector_cols[:], runs[:])

@@ -24,6 +24,7 @@ QUADRANT = 32
 F_PASSES = D // (P * PACK)
 LIST_ROWS = 16
 HALF = I // 2
+QUARTER = I // 4
 BLOCKS = 16
 F_ROWS_FROM = P - F_PASSES * BLOCKS
 C_ROWS_TO = P // 2
@@ -140,22 +141,23 @@ def tile_attend_noisychannel_kernel(tc, hf, hc, vf_words, vf_scales, vc_words, v
         a_term = sb.tile([P, I], F32, name="a_term")
         nc.scalar.activation(a_term[:], a_acc[:], IDENTITY, bias=bias_col[:], scale=wa_col)
 
-        c_words = [sb.tile([P, HALF], U32, name="c_words%d" % h, align_bytes=64) for h in range(2)]
-        for h in range(2):
-            entries = c_list[:, h * HALF // LIST_ROWS : (h + 1) * HALF // LIST_ROWS]
-            nc.vector.tensor_copy(c_words[h][:], c_table[:].indirect(entries))
+        c_words = [sb.tile([P, QUARTER], U32, name="c_words%d" % j, align_bytes=64) for j in range(I // QUARTER)]
+        for j in range(I // QUARTER):
+            entries = c_list[:, j * QUARTER // LIST_ROWS : (j + 1) * QUARTER // LIST_ROWS]
+            nc.vector.tensor_copy(c_words[j][:], c_table[:].indirect(entries))
         for j, (start, width) in enumerate(PIECES):
             cols = slice(start, start + width)
             b_acc = psum.tile([P, width], F32, name="b_acc%d" % j)
-            nc.tensor.matmul_mx(
-                out=b_acc[:],
-                lhsT=hc_codes[:].bitcast(FP8X4),
-                lhsT_scale=hc_plane[:],
-                rhs=c_words[start // HALF][:, start % HALF : start % HALF + width].bitcast(FP8X4),
-                rhs_scale=c_plane[:, cols],
-                start=True,
-                stop=True,
-            )
+            for first in range(0, width, QUARTER):
+                nc.tensor.matmul_mx(
+                    out=b_acc[:, first : first + QUARTER],
+                    lhsT=hc_codes[:].bitcast(FP8X4),
+                    lhsT_scale=hc_plane[:],
+                    rhs=c_words[(start + first) // QUARTER][:].bitcast(FP8X4),
+                    rhs_scale=c_plane[:, start + first : start + first + QUARTER],
+                    start=True,
+                    stop=True,
+                )
             y = dma_tile([P, width], F32, "y%d" % j)
             nc.vector.scalar_tensor_tensor(y[:], b_acc[:], wb_col, a_term[:, cols], MULT, ADD)
             (nc.scalar if j % 2 else nc.sync).dma_start(out[:, cols], y[:])

from contextlib import ExitStack

import concourse.mybir as mybir

D, K, T, I, Q = 1024, 512, 2048, 512, 128
FLOPS = 2 * Q * I * (D + K)

F32 = mybir.dt.float32
BF16 = mybir.dt.bfloat16
I32 = mybir.dt.int32
U32 = mybir.dt.uint32
U16 = mybir.dt.uint16
U8 = mybir.dt.uint8
FP8X4 = mybir.dt.float8_e4m3fn_x4
FP4X4 = mybir.dt.float4_e2m1fn_x4
MULT = mybir.AluOpType.mult
ADD = mybir.AluOpType.add
IDENTITY = mybir.ActivationFunctionType.Identity

P = 128
DMA_ALIGN = 2048
PACK = 4
QUADRANT = 32
F_PASSES = D // (P * PACK)
LIST_ROWS = 16
HALF = I // 2
QUARTER = I // 4
BLOCKS = 16
F_ROWS_FROM = P - F_PASSES * BLOCKS
C_ROWS_TO = P // 2
C_ROWS_FROM = C_ROWS_TO - BLOCKS
C_FIRST = T // 4
PLANE_ROWS = 4
QUADRANT_ORDER = (0, 2, 1, 3)
PIECES = ((0, HALF), (HALF, HALF // 2), (HALF + HALF // 2, HALF // 2))


def cast_and_interleave(nc, grouped, raw):
    nc.scalar.copy(
        out=grouped.rearrange("p (c i) t -> p c t i", i=4),
        in_=raw.rearrange("p t (c i) -> p c t i", i=4),
    )


def tile_attend_noisychannel_kernel(tc, hf, hc, vf_words, vf_scales, vc_words, vc_scales, la, lb, wa, wb, offs, offs2, out):
    nc = tc.nc
    with ExitStack() as ctx:
        moved = ctx.enter_context(tc.tile_pool(name="moved", bufs=1))
        sb = ctx.enter_context(tc.tile_pool(name="sb", bufs=1))
        psum = ctx.enter_context(tc.psum_pool(name="psum", bufs=1))

        def dma_tile(shape, dtype, name):
            return moved.tile(shape, dtype, name=name, tag=name, align_bytes=DMA_ALIGN)

        f_list = dma_tile([P, I // LIST_ROWS], U16, "f_list")
        c_list = dma_tile([P, I // LIST_ROWS], U16, "c_list")
        f_scale_table = dma_tile([P, T], U8, "f_scale_table")
        c_scale_table = dma_tile([P, T], U8, "c_scale_table")
        f_tables = [dma_tile([P, T], U16, "f_table%d" % z) for z in range(F_PASSES)]
        c_table = dma_tile([P, T], U32, "c_table")
        hf_raw = dma_tile([P, F_PASSES, PACK, Q], F32, "hf_raw")
        hc_raw = dma_tile([P, PACK, Q], F32, "hc_raw")
        f_scale_rows = dma_tile([P, I], U8, "f_scale_rows")
        c_scale_rows = dma_tile([P, I], U8, "c_scale_rows")
        f_planes = dma_tile([P, F_PASSES * I], U8, "f_planes")
        c_plane = dma_tile([P, I], U8, "c_plane")
        runs = dma_tile([P, QUADRANT], F32, "runs")

        nc.vector.memset(runs[:], 0.0)
        nc.vector.memset(f_scale_table[0:F_ROWS_FROM, :].bitcast(I32), 0)
        nc.vector.memset(c_scale_table[0:C_ROWS_FROM, :].bitcast(I32), 0)
        nc.vector.memset(c_scale_table[C_ROWS_TO:P, :].bitcast(I32), 0)
        run_rows = [vector.rearrange("(g i) o -> g (i o)", i=QUADRANT) for vector in (wa, wb, la, lb)]
        c_words_in = vc_words[0].rearrange("p c t -> p (c t)").bitcast(I32)

        nc.sync.dma_start(f_list[:], offs)
        nc.scalar.dma_start(f_scale_table[F_ROWS_FROM:P, :].bitcast(I32), vf_scales.rearrange("z f c -> f z c").bitcast(I32))
        nc.sync.dma_start(f_tables[0][:].bitcast(I32), vf_words[0].bitcast(I32))
        nc.scalar.dma_start(c_scale_table[C_ROWS_FROM:C_ROWS_TO, :].bitcast(I32), vc_scales[0].bitcast(I32))
        nc.sync.dma_start(c_list[:], offs2)
        for j in (0, 1):
            nc.sync.dma_start(runs[j:P:QUADRANT, :], run_rows[j])
        nc.sync.dma_start(hf_raw[:], hf.rearrange("(z p t) q -> p z t q", z=F_PASSES, t=PACK))
        nc.sync.dma_start(runs[2:P:QUADRANT, :], run_rows[2])
        nc.sync.dma_start(f_tables[1][:].bitcast(I32), vf_words[1].bitcast(I32))
        nc.sync.dma_start(hc_raw[:], hc.rearrange("(p t) q -> p t q", t=PACK))
        nc.sync.dma_start(c_table[:, 0:C_FIRST].bitcast(I32), c_words_in[:, 0:C_FIRST])
        nc.gpsimd.dma_start(runs[3:P:QUADRANT, :], run_rows[3])

        nc.vector.tensor_copy(f_scale_rows[:], f_scale_table[:].indirect(f_list[:]))
        for g in QUADRANT_ORDER:
            first = F_ROWS_FROM + PLANE_ROWS * F_PASSES * g
            nc.sync.dma_start(
                f_planes[QUADRANT * g : QUADRANT * g + PLANE_ROWS, :].bitcast(I32),
                f_scale_rows[first : first + PLANE_ROWS * F_PASSES, :].bitcast(I32),
            )
        nc.sync.dma_start(c_table[:, C_FIRST:T].bitcast(I32), c_words_in[:, C_FIRST:T])
        nc.vector.tensor_copy(c_scale_rows[:], c_scale_table[:].indirect(c_list[:]))
        for r in range(PLANE_ROWS):
            nc.sync.dma_start(
                c_plane[r:P:QUADRANT, :].bitcast(I32),
                c_scale_rows[C_ROWS_FROM + r : C_ROWS_TO : PLANE_ROWS, :].bitcast(I32),
            )
        f_words = [sb.tile([P, I], U16, name="f_words%d" % z, align_bytes=64) for z in range(F_PASSES)]
        for z in range(F_PASSES):
            nc.vector.tensor_copy(f_words[z][:], f_tables[z][:].indirect(f_list[:]))

        hf_grouped = sb.tile([P, F_PASSES, Q, PACK], BF16, name="hf_grouped", tag="hf_grouped", align_bytes=64)
        hc_grouped = sb.tile([P, Q, PACK], BF16, name="hc_grouped", align_bytes=64)
        for z in range(F_PASSES):
            cast_and_interleave(nc, hf_grouped[:, z], hf_raw[:, z])
        cast_and_interleave(nc, hc_grouped[:], hc_raw[:])
        hf_codes = sb.tile([P, F_PASSES * Q], U32, name="hf_codes", align_bytes=64)
        hf_plane = sb.tile([P, F_PASSES * Q], U8, name="hf_plane", align_bytes=64)
        hc_codes = sb.tile([P, Q], U32, name="hc_codes", align_bytes=64)
        hc_plane = sb.tile([P, Q], U8, name="hc_plane", align_bytes=64)
        nc.vector.quantize_mx(hf_codes[:].bitcast(FP8X4), hf_plane[:], hf_grouped[:].rearrange("p z q t -> p (z q t)"))
        nc.vector.quantize_mx(hc_codes[:].bitcast(FP8X4), hc_plane[:], hc_grouped[:].rearrange("p q t -> p (q t)"))

        a_acc = psum.tile([P, I], F32, name="a_acc")
        for z in range(F_PASSES):
            nc.tensor.matmul_mx(
                out=a_acc[:],
                lhsT=hf_codes[:, z * Q : (z + 1) * Q].bitcast(FP8X4),
                lhsT_scale=hf_plane[:, z * Q : (z + 1) * Q],
                rhs=f_words[z][:].bitcast(FP4X4),
                rhs_scale=f_planes[:, z * I : (z + 1) * I],
                start=(z == 0),
                stop=(z == F_PASSES - 1),
            )

        vector_cols = sb.tile([P, QUADRANT], F32, name="vector_cols", tag="hf_grouped", align_bytes=64)
        nc.vector.transpose(vector_cols[:], runs[:])
        wa_col, wb_col, la_col, lb_col = (vector_cols[:, j : j + 1] for j in range(len(run_rows)))
        wb_lb = moved.tile([P, 1], F32, name="wb_lb", tag="hc_raw", align_bytes=DMA_ALIGN)
        weighted_sums = sb.tile([P, 1], F32, name="weighted_sums")
        bias_col = sb.tile([P, 1], F32, name="bias_col")
        nc.scalar.activation(wb_lb[:], lb_col, IDENTITY, scale=wb_col)
        nc.scalar.activation(weighted_sums[:], la_col, IDENTITY, bias=wb_lb[:], scale=wa_col)
        nc.scalar.activation(bias_col[:], weighted_sums[:], IDENTITY, scale=-1.0)
        a_term = sb.tile([P, I], F32, name="a_term")
        nc.scalar.activation(a_term[:], a_acc[:], IDENTITY, bias=bias_col[:], scale=wa_col)

        c_words = [sb.tile([P, QUARTER], U32, name="c_words%d" % j, align_bytes=64) for j in range(I // QUARTER)]
        for j in range(I // QUARTER):
            entries = c_list[:, j * QUARTER // LIST_ROWS : (j + 1) * QUARTER // LIST_ROWS]
            nc.vector.tensor_copy(c_words[j][:], c_table[:].indirect(entries))
        for j, (start, width) in enumerate(PIECES):
            cols = slice(start, start + width)
            b_acc = psum.tile([P, width], F32, name="b_acc%d" % j)
            for first in range(0, width, QUARTER):
                nc.tensor.matmul_mx(
                    out=b_acc[:, first : first + QUARTER],
                    lhsT=hc_codes[:].bitcast(FP8X4),
                    lhsT_scale=hc_plane[:],
                    rhs=c_words[(start + first) // QUARTER][:].bitcast(FP8X4),
                    rhs_scale=c_plane[:, start + first : start + first + QUARTER],
                    start=True,
                    stop=True,
                )
            y = dma_tile([P, width], F32, "y%d" % j)
            nc.vector.scalar_tensor_tensor(y[:], b_acc[:], wb_col, a_term[:, cols], MULT, ADD)
            (nc.scalar if j % 2 else nc.sync).dma_start(out[:, cols], y[:])
